import numpy as np
import ml_dtypes


def mxq(x, axis, fmt="e4m3"):
    dtype, down = {"e4m3": (ml_dtypes.float8_e4m3fn, 7), "e5m2": (ml_dtypes.float8_e5m2, 14)}[fmt]
    v = np.moveaxis(np.asarray(x, np.float32).astype(ml_dtypes.bfloat16).astype(np.float64), axis, -1)
    blocks = v.reshape(v.shape[:-1] + (-1, 32))
    amax = np.abs(blocks).max(-1, keepdims=True)
    byte = np.maximum(np.where(amax > 0, np.frexp(amax)[1] - 1 + 127, 0) - down, 1)
    scale = np.exp2(byte - 127.0)
    codes = (blocks / scale).astype(np.float32).astype(dtype).astype(np.float64)
    return np.moveaxis((codes * scale).reshape(v.shape), -1, axis)


WIDE = False


def mx_kscale(k):
    if not WIDE:
        return np.ones(k)
    levels = np.array([10, -10, 5, -5, 0])
    if k % 512:
        return np.exp2(np.random.permutation(np.resize(levels, k // 32))).repeat(32)
    a = np.empty((k // 512, 16))
    for p in range(k // 512):
        a[p, :8] = np.random.permutation(np.resize(levels, 8))
        for g in range(8):
            far = levels[np.abs(levels - a[p, g]) >= 10]
            a[p, g + 8] = far[np.random.randint(len(far))]
    return np.exp2(a.ravel()).repeat(32)


def f64(x):
    return np.asarray(x).astype(np.float64)


def striped(idx):
    return np.tile(idx.reshape(-1, 16).T, (8, 1)).astype(np.uint16)


def unstriped(offs):
    return offs[:16].T.reshape(-1).astype(np.int64)


def pack_weight(w):
    k, n = w.shape
    w = f64(np.asarray(w, np.float32).astype(ml_dtypes.bfloat16)).reshape(k // 32, 32, n)
    amax = np.abs(w).max(1)
    byte = np.clip(np.where(amax > 0, np.frexp(amax)[1] - 1 + 127 - 7, 1), 1, 254)
    scaled = (w * np.exp2(127.0 - byte)[:, None, :]).reshape(k, n).astype(np.float32)
    words = np.ascontiguousarray(scaled.reshape(k // 512, 128, 4, n).transpose(0, 1, 3, 2)).astype(ml_dtypes.float8_e4m3fn).view(np.uint8)
    return words, np.ascontiguousarray(byte.astype(np.uint8).reshape(k // 512, 16, n))


def unpack_weight(words, scales):
    g, p, n, _ = words.shape
    vals = np.ascontiguousarray(words).view(ml_dtypes.float8_e4m3fn).astype(np.float64) * np.repeat(np.exp2(scales.astype(np.float64) - 127.0), 8, axis=1)[..., None]
    return vals.transpose(0, 1, 3, 2).reshape(g * 512, n)


K, T, S, V, U, D = 512, 1024, 512, 512, 256, 4
P = 2 ** 7


def setup_inputs():
    n = np.random.standard_normal
    s = mx_kscale(K)[:, None]
    packed_xT = pack_weight(n((K, T)) * s)
    return {
        "x_words": packed_xT[0],
        "x_scales": packed_xT[1],
        "hT": (n((K, V)) / np.sqrt(K) / s).astype(np.float32),
        "turn": (np.tile(np.where(np.random.uniform(size=(D, 1, U)) < 0.5, 1.0, -1.0), (1, P, 1))).astype(np.float32),
        "offs": striped(np.random.permutation(T)[:S]),
        "pos1": striped(np.random.randint(0, S, U)),
        "pos2": striped(np.random.randint(0, S, U)),
        "pos3": striped(np.random.randint(0, S, U)),
        "pos4": striped(np.random.randint(0, S, U)),
    }


def reference(x_words, x_scales, hT, turn, offs, pos1, pos2, pos3, pos4):
    hTq = mxq(f64(hT), 0, "e4m3")
    xq = unpack_weight(x_words, x_scales)[:, unstriped(offs)]
    y = hTq.T @ xq
    z0 = y[:, unstriped(pos1)] * f64(turn)[0, :1]
    z1 = y[:, unstriped(pos2)] * f64(turn)[1, :1]
    z2 = y[:, unstriped(pos3)] * f64(turn)[2, :1]
    z3 = y[:, unstriped(pos4)] * f64(turn)[3, :1]
    return np.log(np.exp(-1.0 * z0) + 1.0) + np.log(np.exp(-1.0 * z1) + 1.0) + np.log(np.exp(-1.0 * z2) + 1.0) + np.log(np.exp(-1.0 * z3) + 1.0)

@@ -1,0 +1,136 @@
+from contextlib import ExitStack
+
+import concourse.mybir as mybir
+from concourse.masks import make_identity
+
+K, T, S, V, U, D = 512, 1024, 512, 512, 256, 4
+P = 128
+PACK = 4
+BLOCKS = V // P
+HALVES = U // P
+FLOPS = 2 * K * V * S
+
+F32 = mybir.dt.float32
+BF16 = mybir.dt.bfloat16
+I32 = mybir.dt.int32
+U32 = mybir.dt.uint32
+U16 = mybir.dt.uint16
+U8 = mybir.dt.uint8
+FP8X4 = mybir.dt.float8_e4m3fn_x4
+ACT = mybir.ActivationFunctionType
+ALU = mybir.AluOpType
+
+
+def tile_picked_yhs_nll_p_kernel(tc, x_words, x_scales, hT, turn, offs, pos1, pos2, pos3, pos4, out):
+    nc = tc.nc
+    with ExitStack() as ctx:
+        lists = ctx.enter_context(tc.tile_pool(name="lists", bufs=1))
+        keep = ctx.enter_context(tc.tile_pool(name="keep", bufs=1))
+        psum = ctx.enter_context(tc.psum_pool(name="psum", bufs=1))
+
+        table_scales = keep.tile([P, T], U8, name="table_scales", align_bytes=64)
+        nc.vector.memset(table_scales[:].bitcast(I32), 0)
+        zero = keep.tile([P, 1], F32, name="zero")
+        nc.vector.memset(zero[:], 0.0)
+        half = keep.tile([P, 1], F32, name="half")
+        nc.scalar.activation(half[:], zero[:], ACT.Sigmoid)
+
+        table_words = keep.tile([P, T], U32, name="table_words", align_bytes=64)
+        picked = lists.tile([P, S // 16], U16, name="picked")
+        nc.sync.dma_start(picked[:], offs)
+        for q in range(4):
+            nc.sync.dma_start(
+                table_scales[32 * q : 32 * q + 4, :].bitcast(I32),
+                x_scales[0, 4 * q : 4 * q + 4, :].bitcast(I32),
+            )
+        nc.sync.dma_start(table_words[:].bitcast(I32), x_words[0].rearrange("p n t -> p (n t)").bitcast(I32))
+        h_rows = hT.rearrange("(p j) t -> p j t", j=PACK)
+        h_raw = [keep.tile([P, PACK, P], F32, name="h_raw%d" % b) for b in range(BLOCKS)]
+        paths = [lists.tile([P, U // 16], U16, name="path%d" % d) for d in range(D)]
+        signs = [keep.tile([P, U], F32, name="sign%d" % d) for d in range(D)]
+        nc.sync.dma_start(h_raw[0][:], h_rows[:, :, 0:P])
+        nc.sync.dma_start(h_raw[1][:], h_rows[:, :, P : 2 * P])
+        for d, pos in enumerate((pos1, pos2, pos3, pos4)):
+            nc.sync.dma_start(paths[d][:], pos)
+            nc.sync.dma_start(signs[d][:], turn[d])
+        for b in range(2, BLOCKS):
+            nc.sync.dma_start(h_raw[b][:], h_rows[:, :, b * P : (b + 1) * P])
+
+        ident = keep.tile([P, P], F32, name="ident")
+        make_identity(nc, ident[:])
+
+        node_scales = keep.tile([P, S], U8, name="node_scales", align_bytes=64)
+        nc.vector.tensor_copy(node_scales[:], table_scales[:].indirect(picked[:]))
+        node_words = keep.tile([P, S], U32, name="node_words", align_bytes=64)
+        for i in range(2):
+            nc.vector.tensor_copy(node_words[:, i * 256 : (i + 1) * 256], table_words[:].indirect(picked[:, i * 16 : (i + 1) * 16]))
+
+        neg_y = []
+        for b in range(BLOCKS):
+            grouped = keep.tile([P, P, PACK], BF16, name="grouped%d" % b, align_bytes=64)
+            nc.scalar.copy(
+                grouped[:].rearrange("p (c i) j -> p c j i", i=4),
+                h_raw[b][:].rearrange("p j (c i) -> p c j i", i=4),
+            )
+            h_words = keep.tile([P, P], U32, name="h_words%d" % b, align_bytes=64)
+            h_scales = keep.tile([P, P], U8, name="h_scales%d" % b, align_bytes=64)
+            nc.vector.quantize_mx(
+                out=h_words[:].bitcast(FP8X4),
+                scales=h_scales[:],
+                in_=grouped[:].rearrange("p t j -> p (t j)"),
+            )
+            window = keep.tile([P, S], F32, name="neg_y%d" % b)
+            pieces = 2 if b == 0 else 1
+            width = S // pieces
+            for i in range(pieces):
+                cols = slice(i * width, (i + 1) * width)
+                y_bank = psum.tile([P, width], F32, name="y_bank", tag="y_bank", bufs=2)
+                nc.tensor.matmul_mx(
+                    out=y_bank[:],
+                    lhsT=h_words[:].bitcast(FP8X4),
+                    lhsT_scale=h_scales[:],
+                    rhs=node_words[:, cols].bitcast(FP8X4),
+                    rhs_scale=node_scales[:, cols],
+                    start=True,
+                    stop=True,
+                )
+                nc.scalar.activation(window[:, cols], y_bank[:], ACT.Copy, scale=-1.0)
+            neg_y.append(window)
+
+        pairs = keep.tile([P, BLOCKS, 2, U], F32, name="pairs")
+        ramp_banks = [psum.tile([P, 2, U], F32, name="ramp%d" % i) for i in range(BLOCKS // 2)]
+        for b in range(BLOCKS):
+            x = keep.tile([P, D, U], F32, name="x%d" % b)
+            mag = keep.tile([P, D, U], F32, name="mag%d" % b)
+            sig = keep.tile([P, D, U], F32, name="sig%d" % b)
+            sums = [psum.tile([P, P], F32, name="sum%d" % h, tag="sum%d" % h, bufs=2) for h in range(HALVES)]
+            step = 1 if b == BLOCKS - 1 else 2
+            for d0 in range(0, D, step):
+                for d in range(d0, d0 + step):
+                    nc.vector.tensor_tensor(x[:, d, :], neg_y[b][:].indirect(paths[d][:]), signs[d][:], ALU.mult)
+                nc.scalar.activation(mag[:, d0 : d0 + step, :], x[:, d0 : d0 + step, :], ACT.Abs)
+                nc.scalar.activation(sig[:, d0 : d0 + step, :], mag[:, d0 : d0 + step, :], ACT.Sigmoid)
+                for d in range(d0, d0 + step):
+                    for h in range(HALVES):
+                        cols = slice(h * P, (h + 1) * P)
+                        nc.tensor.matmul(sums[h][:], x[:, d, cols], ident[:], start=(d == 0), stop=False, is_transpose=True)
+                        nc.tensor.matmul(sums[h][:], mag[:, d, cols], ident[:], start=False, stop=(d == D - 1), is_transpose=True)
+                if (d0 + step) % 2 == 0:
+                    e = (d0 + step) // 2 - 1
+                    nc.vector.tensor_tensor(pairs[:, b, e, :], sig[:, 2 * e, :], sig[:, 2 * e + 1, :], ALU.mult)
+            turned = keep.tile([P, HALVES, P], F32, name="turned%d" % b)
+            for h in range(HALVES):
+                if b == BLOCKS - 1:
+                    nc.vector.tensor_copy(turned[:, h, :], sums[h][:])
+                else:
+                    nc.scalar.copy(turned[:, h, :], sums[h][:])
+                nc.tensor.transpose(ramp_banks[b // 2][:, b % 2, h * P : (h + 1) * P], turned[:, h, :], ident[:])
+
+        prod = keep.tile([P, BLOCKS, U], F32, name="prod")
+        nc.vector.tensor_tensor(prod[:], pairs[:, :, 0, :], pairs[:, :, 1, :], ALU.mult)
+        for b in range(BLOCKS):
+            logs = keep.tile([P, U], F32, name="logs%d" % b)
+            nc.scalar.activation(logs[:], prod[:, b, :], ACT.Ln)
+            res = keep.tile([P, U], F32, name="res%d" % b)
+            nc.vector.scalar_tensor_tensor(res[:], ramp_banks[b // 2][:, b % 2, :], half[:], logs[:], ALU.mult, ALU.subtract)
+            nc.sync.dma_start(out[b * P : (b + 1) * P, :], res[:])

@@ -28,109 +28,190 @@ def tile_picked_yhs_nll_p_kernel(tc, x_words, x_scales, hT, turn, offs, pos1, po
         keep = ctx.enter_context(tc.tile_pool(name="keep", bufs=1))
         psum = ctx.enter_context(tc.psum_pool(name="psum", bufs=1))
 
+        scale_rows = keep.tile([P, T // 4], I32, name="scale_rows")
+        picked = lists.tile([P, S // 16], U16, name="picked")
+        nc.sync.dma_start(picked[:], offs)
+        for q in range(4):
+            queue = nc.sync if q == 0 else nc.scalar
+            queue.dma_start(scale_rows[32 * q : 32 * q + 4, :], x_scales[0, 4 * q : 4 * q + 4, :].bitcast(I32))
         table_scales = keep.tile([P, T], U8, name="table_scales", align_bytes=64)
         nc.vector.memset(table_scales[:].bitcast(I32), 0)
+        for q in range(4):
+            rows = slice(32 * q, 32 * q + 4)
+            nc.vector.tensor_copy(table_scales[rows, :].bitcast(I32), scale_rows[rows, :])
         zero = keep.tile([P, 1], F32, name="zero")
         nc.vector.memset(zero[:], 0.0)
         half = keep.tile([P, 1], F32, name="half")
         nc.scalar.activation(half[:], zero[:], ACT.Sigmoid)
 
-        table_words = keep.tile([P, T], U32, name="table_words", align_bytes=64)
-        picked = lists.tile([P, S // 16], U16, name="picked")
-        nc.sync.dma_start(picked[:], offs)
-        for q in range(4):
-            nc.sync.dma_start(
-                table_scales[32 * q : 32 * q + 4, :].bitcast(I32),
-                x_scales[0, 4 * q : 4 * q + 4, :].bitcast(I32),
-            )
-        nc.sync.dma_start(table_words[:].bitcast(I32), x_words[0].rearrange("p n t -> p (n t)").bitcast(I32))
         h_rows = hT.rearrange("(p j) t -> p j t", j=PACK)
-        h_raw = [keep.tile([P, PACK, P], F32, name="h_raw%d" % b) for b in range(BLOCKS)]
+        groups = ((0, 1), (1, 1), (2, 2))
+        h_raw = [keep.tile([P, PACK, n * P], F32, name="h_raw%d" % b) for b, n in groups]
         paths = [lists.tile([P, U // 16], U16, name="path%d" % d) for d in range(D)]
-        signs = [keep.tile([P, U], F32, name="sign%d" % d) for d in range(D)]
-        nc.sync.dma_start(h_raw[0][:], h_rows[:, :, 0:P])
-        nc.sync.dma_start(h_raw[1][:], h_rows[:, :, P : 2 * P])
-        for d, pos in enumerate((pos1, pos2, pos3, pos4)):
-            nc.sync.dma_start(paths[d][:], pos)
-            nc.sync.dma_start(signs[d][:], turn[d])
-        for b in range(2, BLOCKS):
-            nc.sync.dma_start(h_raw[b][:], h_rows[:, :, b * P : (b + 1) * P])
+        signs = keep.tile([P, D, U], F32, name="signs")
+        table_words = keep.tile([P, T], U32, name="table_words", align_bytes=64)
+        poss = (pos1, pos2, pos3, pos4)
+
+        def load_h(g):
+            b, n = groups[g]
+            nc.sync.dma_start(h_raw[g][:], h_rows[:, :, b * P : (b + n) * P])
+
+        def load_path(d):
+            nc.sync.dma_start(paths[d][:], poss[d])
+
+        def load_signs():
+            nc.sync.dma_start(signs[:], turn.rearrange("d p u -> p d u"))
+
+        def load_words():
+            nc.sync.dma_start(table_words[:].bitcast(I32), x_words[0].rearrange("p n t -> p (n t)").bitcast(I32))
+
+        load_h(0)
+        load_words()
+        load_h(1)
+        for d in range(D):
+            load_path(d)
+        load_signs()
+        load_h(2)
 
         ident = keep.tile([P, P], F32, name="ident")
         make_identity(nc, ident[:])
 
         node_scales = keep.tile([P, S], U8, name="node_scales", align_bytes=64)
-        nc.vector.tensor_copy(node_scales[:], table_scales[:].indirect(picked[:]))
         node_words = keep.tile([P, S], U32, name="node_words", align_bytes=64)
-        for i in range(2):
-            nc.vector.tensor_copy(node_words[:, i * 256 : (i + 1) * 256], table_words[:].indirect(picked[:, i * 16 : (i + 1) * 16]))
+        h_words = [keep.tile([P, n * P], U32, name="h_words%d" % b, align_bytes=64) for b, n in groups]
+        h_scales = [keep.tile([P, n * P], U8, name="h_scales%d" % b, align_bytes=64) for b, n in groups]
+        neg_y = [keep.tile([P, S], F32, name="neg_y%d" % b) for b in range(BLOCKS)]
+        pairs = keep.tile([P, BLOCKS, 2, U], F32, name="pairs")
+        prod = keep.tile([P, BLOCKS, U], F32, name="prod")
+        logs = keep.tile([P, BLOCKS, U], F32, name="logs")
+        ramp_banks = [psum.tile([P, 2, U], F32, name="ramp%d" % i) for i in range(BLOCKS // 2)]
+        xs = [keep.tile([P, D, U], F32, name="x%d" % b) for b in range(BLOCKS)]
+        mags = [keep.tile([P, D, U], F32, name="mag%d" % b) for b in range(BLOCKS)]
+        sigs = keep.tile([P, BLOCKS, 2, 2, U], F32, name="sigs")
+        sums = {}
 
-        neg_y = []
-        for b in range(BLOCKS):
-            grouped = keep.tile([P, P, PACK], BF16, name="grouped%d" % b, align_bytes=64)
-            nc.scalar.copy(
-                grouped[:].rearrange("p (c i) j -> p c j i", i=4),
-                h_raw[b][:].rearrange("p j (c i) -> p c j i", i=4),
-            )
-            h_words = keep.tile([P, P], U32, name="h_words%d" % b, align_bytes=64)
-            h_scales = keep.tile([P, P], U8, name="h_scales%d" % b, align_bytes=64)
+        def quantise(g, on_vector):
+            b, n = groups[g]
+            grouped = keep.tile([P, n * P, PACK], BF16, name="grouped%d" % b, align_bytes=64)
+            dst = grouped[:].rearrange("p (c i) j -> p c j i", i=4)
+            src = h_raw[g][:].rearrange("p j (c i) -> p c j i", i=4)
+            if on_vector:
+                nc.vector.tensor_copy(dst, src)
+            else:
+                nc.scalar.copy(dst, src)
             nc.vector.quantize_mx(
-                out=h_words[:].bitcast(FP8X4),
-                scales=h_scales[:],
+                out=h_words[g][:].bitcast(FP8X4),
+                scales=h_scales[g][:],
                 in_=grouped[:].rearrange("p t j -> p (t j)"),
             )
-            window = keep.tile([P, S], F32, name="neg_y%d" % b)
-            pieces = 2 if b == 0 else 1
+
+        def scores(b, pieces):
+            g = max(i for i, (first, n) in enumerate(groups) if first <= b)
+            own = slice((b - groups[g][0]) * P, (b - groups[g][0] + 1) * P)
             width = S // pieces
             for i in range(pieces):
                 cols = slice(i * width, (i + 1) * width)
                 y_bank = psum.tile([P, width], F32, name="y_bank", tag="y_bank", bufs=2)
                 nc.tensor.matmul_mx(
                     out=y_bank[:],
-                    lhsT=h_words[:].bitcast(FP8X4),
-                    lhsT_scale=h_scales[:],
+                    lhsT=h_words[g][:, own].bitcast(FP8X4),
+                    lhsT_scale=h_scales[g][:, own],
                     rhs=node_words[:, cols].bitcast(FP8X4),
                     rhs_scale=node_scales[:, cols],
                     start=True,
                     stop=True,
                 )
-                nc.scalar.activation(window[:, cols], y_bank[:], ACT.Copy, scale=-1.0)
-            neg_y.append(window)
+                nc.scalar.activation(neg_y[b][:, cols], y_bank[:], ACT.Copy, scale=-1.0)
 
-        pairs = keep.tile([P, BLOCKS, 2, U], F32, name="pairs")
-        ramp_banks = [psum.tile([P, 2, U], F32, name="ramp%d" % i) for i in range(BLOCKS // 2)]
-        for b in range(BLOCKS):
-            x = keep.tile([P, D, U], F32, name="x%d" % b)
-            mag = keep.tile([P, D, U], F32, name="mag%d" % b)
-            sig = keep.tile([P, D, U], F32, name="sig%d" % b)
-            sums = [psum.tile([P, P], F32, name="sum%d" % h, tag="sum%d" % h, bufs=2) for h in range(HALVES)]
-            step = 1 if b == BLOCKS - 1 else 2
-            for d0 in range(0, D, step):
-                for d in range(d0, d0 + step):
-                    nc.vector.tensor_tensor(x[:, d, :], neg_y[b][:].indirect(paths[d][:]), signs[d][:], ALU.mult)
-                nc.scalar.activation(mag[:, d0 : d0 + step, :], x[:, d0 : d0 + step, :], ACT.Abs)
-                nc.scalar.activation(sig[:, d0 : d0 + step, :], mag[:, d0 : d0 + step, :], ACT.Sigmoid)
-                for d in range(d0, d0 + step):
-                    for h in range(HALVES):
-                        cols = slice(h * P, (h + 1) * P)
-                        nc.tensor.matmul(sums[h][:], x[:, d, cols], ident[:], start=(d == 0), stop=False, is_transpose=True)
-                        nc.tensor.matmul(sums[h][:], mag[:, d, cols], ident[:], start=False, stop=(d == D - 1), is_transpose=True)
-                if (d0 + step) % 2 == 0:
-                    e = (d0 + step) // 2 - 1
-                    nc.vector.tensor_tensor(pairs[:, b, e, :], sig[:, 2 * e, :], sig[:, 2 * e + 1, :], ALU.mult)
+        def fetch(b, d0, count):
+            x, mag = xs[b], mags[b]
+            if d0 == 0:
+                sums[b] = [psum.tile([P, P], F32, name="sum%d" % h, tag="sum%d" % h, bufs=2) for h in range(HALVES)]
+            for d in range(d0, d0 + count):
+                nc.vector.tensor_tensor(x[:, d, :], neg_y[b][:].indirect(paths[d][:]), signs[:, d, :], ALU.mult)
+            nc.scalar.activation(mag[:, d0 : d0 + count, :], x[:, d0 : d0 + count, :], ACT.Abs)
+            for d in range(d0, d0 + count):
+                for h in range(HALVES):
+                    cols = slice(h * P, (h + 1) * P)
+                    nc.tensor.matmul(sums[b][h][:], x[:, d, cols], ident[:], start=(d == 0), stop=False, is_transpose=True)
+                    nc.tensor.matmul(sums[b][h][:], mag[:, d, cols], ident[:], start=False, stop=(d == D - 1), is_transpose=True)
+
+        def squash(b, d0, count):
+            sig = sigs[:, b].rearrange("p e f u -> p (e f) u")
+            nc.scalar.activation(sig[:, d0 : d0 + count, :], mags[b][:, d0 : d0 + count, :], ACT.Sigmoid)
+
+        def clock(src, n):
+            c = keep.tile([P, 1], F32, name="clock%d" % n)
+            nc.gpsimd.tensor_copy(c[:], src)
+
+        def pair(b, e0, count):
+            es = slice(e0, e0 + count)
+            nc.vector.tensor_tensor(pairs[:, b, es, :], sigs[:, b, es, 0, :], sigs[:, b, es, 1, :], ALU.mult)
+
+        def product(b0, count):
+            bs = slice(b0, b0 + count)
+            nc.vector.tensor_tensor(prod[:, bs, :], pairs[:, bs, 0, :], pairs[:, bs, 1, :], ALU.mult)
+
+        def turn_back(b, on_vector=False):
             turned = keep.tile([P, HALVES, P], F32, name="turned%d" % b)
             for h in range(HALVES):
-                if b == BLOCKS - 1:
-                    nc.vector.tensor_copy(turned[:, h, :], sums[h][:])
+                if on_vector:
+                    nc.vector.tensor_copy(turned[:, h, :], sums[b][h][:])
                 else:
-                    nc.scalar.copy(turned[:, h, :], sums[h][:])
+                    nc.scalar.copy(turned[:, h, :], sums[b][h][:])
                 nc.tensor.transpose(ramp_banks[b // 2][:, b % 2, h * P : (h + 1) * P], turned[:, h, :], ident[:])
 
-        prod = keep.tile([P, BLOCKS, U], F32, name="prod")
-        nc.vector.tensor_tensor(prod[:], pairs[:, :, 0, :], pairs[:, :, 1, :], ALU.mult)
-        for b in range(BLOCKS):
-            logs = keep.tile([P, U], F32, name="logs%d" % b)
-            nc.scalar.activation(logs[:], prod[:, b, :], ACT.Ln)
+        def log(b0, count):
+            bs = slice(b0, b0 + count)
+            nc.scalar.activation(logs[:, bs, :], prod[:, bs, :], ACT.Ln)
+
+        def finish(b):
             res = keep.tile([P, U], F32, name="res%d" % b)
-            nc.vector.scalar_tensor_tensor(res[:], ramp_banks[b // 2][:, b % 2, :], half[:], logs[:], ALU.mult, ALU.subtract)
+            nc.vector.scalar_tensor_tensor(res[:], ramp_banks[b // 2][:, b % 2, :], half[:], logs[:, b, :], ALU.mult, ALU.subtract)
             nc.sync.dma_start(out[b * P : (b + 1) * P, :], res[:])
+
+        def gather_words(i):
+            nc.vector.tensor_copy(node_words[:, i * 256 : (i + 1) * 256], table_words[:].indirect(picked[:, i * 16 : (i + 1) * 16]))
+
+        nc.vector.tensor_copy(node_scales[:], table_scales[:].indirect(picked[:]))
+        quantise(0, False)
+        gather_words(0)
+        gather_words(1)
+        scores(0, 2)
+        quantise(1, False)
+        scores(1, 1)
+        quantise(2, True)
+        fetch(0, 0, 2)
+        squash(0, 0, 2)
+        fetch(0, 2, 2)
+        scores(2, 1)
+        squash(0, 2, 2)
+        fetch(1, 0, 2)
+        scores(3, 1)
+        squash(1, 0, 2)
+        fetch(1, 2, 2)
+        turn_back(0)
+        squash(1, 2, 2)
+        fetch(2, 0, 2)
+        fetch(2, 2, 2)
+        squash(2, 0, 2)
+        turn_back(1)
+        fetch(3, 0, 2)
+        squash(2, 2, 2)
+        fetch(3, 2, 1)
+        squash(3, 0, 2)
+        fetch(3, 3, 1)
+        squash(3, 2, 1)
+        squash(3, 3, 1)
+        for b in range(BLOCKS - 1):
+            pair(b, 0, 2)
+            product(b, 1)
+        turn_back(2, True)
+        pair(3, 0, 1)
+        pair(3, 1, 1)
+        turn_back(3, True)
+        product(3, 1)
+        for b in range(BLOCKS):
+            log(b, 1)
+        for b in range(BLOCKS):
+            finish(b)

@@ -68,10 +68,10 @@ def tile_picked_yhs_nll_p_kernel(tc, x_words, x_scales, hT, turn, offs, pos1, po
         load_h(0)
         load_words()
         load_h(1)
+        load_h(2)
         for d in range(D):
             load_path(d)
         load_signs()
-        load_h(2)
 
         ident = keep.tile([P, P], F32, name="ident")
         make_identity(nc, ident[:])
@@ -88,7 +88,9 @@ def tile_picked_yhs_nll_p_kernel(tc, x_words, x_scales, hT, turn, offs, pos1, po
         xs = [keep.tile([P, D, U], F32, name="x%d" % b) for b in range(BLOCKS)]
         mags = [keep.tile([P, D, U], F32, name="mag%d" % b) for b in range(BLOCKS)]
         sigs = keep.tile([P, BLOCKS, 2, 2, U], F32, name="sigs")
+        sum_groups = ((0, 2), (2, 1), (3, 1))
         sums = {}
+        word_cuts = (0, 256, 512)
 
         def quantise(g, on_vector):
             b, n = groups[g]
@@ -108,9 +110,10 @@ def tile_picked_yhs_nll_p_kernel(tc, x_words, x_scales, hT, turn, offs, pos1, po
         def scores(b, pieces):
             g = max(i for i, (first, n) in enumerate(groups) if first <= b)
             own = slice((b - groups[g][0]) * P, (b - groups[g][0] + 1) * P)
-            width = S // pieces
-            for i in range(pieces):
-                cols = slice(i * width, (i + 1) * width)
+            cuts = word_cuts if pieces > 1 else (0, S)
+            for i in range(len(cuts) - 1):
+                width = cuts[i + 1] - cuts[i]
+                cols = slice(cuts[i], cuts[i + 1])
                 y_bank = psum.tile([P, width], F32, name="y_bank", tag="y_bank", bufs=2)
                 nc.tensor.matmul_mx(
                     out=y_bank[:],
@@ -125,16 +128,27 @@ def tile_picked_yhs_nll_p_kernel(tc, x_words, x_scales, hT, turn, offs, pos1, po
 
         def fetch(b, d0, count):
             x, mag = xs[b], mags[b]
-            if d0 == 0:
-                sums[b] = [psum.tile([P, P], F32, name="sum%d" % h, tag="sum%d" % h, bufs=2) for h in range(HALVES)]
+            i = max(j for j, (first, n) in enumerate(sum_groups) if first <= b)
+            first, n = sum_groups[i]
+            if d0 == 0 and b == first:
+                if i == len(sum_groups) - 1:
+                    sums[i] = [psum.tile([P, n, P], F32, name="sum_last", tag="y_bank", bufs=2) for h in range(HALVES)]
+                else:
+                    sums[i] = [psum.tile([P, n, P], F32, name="sum%d_%d" % (i, h)) for h in range(HALVES)]
             for d in range(d0, d0 + count):
                 nc.vector.tensor_tensor(x[:, d, :], neg_y[b][:].indirect(paths[d][:]), signs[:, d, :], ALU.mult)
             nc.scalar.activation(mag[:, d0 : d0 + count, :], x[:, d0 : d0 + count, :], ACT.Abs)
-            for d in range(d0, d0 + count):
-                for h in range(HALVES):
-                    cols = slice(h * P, (h + 1) * P)
-                    nc.tensor.matmul(sums[b][h][:], x[:, d, cols], ident[:], start=(d == 0), stop=False, is_transpose=True)
-                    nc.tensor.matmul(sums[b][h][:], mag[:, d, cols], ident[:], start=False, stop=(d == D - 1), is_transpose=True)
+            for terms in (x, mag):
+                for d in range(d0, d0 + count):
+                    for h in range(HALVES):
+                        nc.tensor.matmul(
+                            sums[i][h][:, b - first, :],
+                            terms[:, d, h * P : (h + 1) * P],
+                            ident[:],
+                            start=(terms is x and d == 0),
+                            stop=(terms is mag and d == D - 1),
+                            is_transpose=True,
+                        )
 
         def squash(b, d0, count):
             sig = sigs[:, b].rearrange("p e f u -> p (e f) u")
@@ -148,70 +162,83 @@ def tile_picked_yhs_nll_p_kernel(tc, x_words, x_scales, hT, turn, offs, pos1, po
             es = slice(e0, e0 + count)
             nc.vector.tensor_tensor(pairs[:, b, es, :], sigs[:, b, es, 0, :], sigs[:, b, es, 1, :], ALU.mult)
 
+        def pair_blocks(b0, count):
+            bs = slice(b0, b0 + count)
+            nc.vector.tensor_tensor(pairs[:, bs], sigs[:, bs, :, 0, :], sigs[:, bs, :, 1, :], ALU.mult)
+
         def product(b0, count):
             bs = slice(b0, b0 + count)
             nc.vector.tensor_tensor(prod[:, bs, :], pairs[:, bs, 0, :], pairs[:, bs, 1, :], ALU.mult)
 
-        def turn_back(b, on_vector=False):
-            turned = keep.tile([P, HALVES, P], F32, name="turned%d" % b)
+        def turn_back(i, on_vector=False):
+            first, n = sum_groups[i]
+            turned = keep.tile([P, HALVES, n, P], F32, name="turned%d" % i)
             for h in range(HALVES):
                 if on_vector:
-                    nc.vector.tensor_copy(turned[:, h, :], sums[b][h][:])
+                    nc.vector.tensor_copy(turned[:, h], sums[i][h][:])
                 else:
-                    nc.scalar.copy(turned[:, h, :], sums[b][h][:])
-                nc.tensor.transpose(ramp_banks[b // 2][:, b % 2, h * P : (h + 1) * P], turned[:, h, :], ident[:])
+                    nc.scalar.copy(turned[:, h], sums[i][h][:])
+                for k in range(n):
+                    b = first + k
+                    nc.tensor.transpose(ramp_banks[b // 2][:, b % 2, h * P : (h + 1) * P], turned[:, h, k, :], ident[:])
 
         def log(b0, count):
             bs = slice(b0, b0 + count)
             nc.scalar.activation(logs[:, bs, :], prod[:, bs, :], ACT.Ln)
 
-        def finish(b):
-            res = keep.tile([P, U], F32, name="res%d" % b)
-            nc.vector.scalar_tensor_tensor(res[:], ramp_banks[b // 2][:, b % 2, :], half[:], logs[:, b, :], ALU.mult, ALU.subtract)
-            nc.sync.dma_start(out[b * P : (b + 1) * P, :], res[:])
+        def finish(b0, count):
+            res = keep.tile([P, count, U], F32, name="res%d" % b0)
+            ks = slice(b0 % 2, b0 % 2 + count)
+            nc.vector.scalar_tensor_tensor(res[:], ramp_banks[b0 // 2][:, ks, :], half[:], logs[:, b0 : b0 + count, :], ALU.mult, ALU.subtract)
+            nc.sync.dma_start(out[b0 * P : (b0 + count) * P, :].rearrange("(b p) u -> p b u", p=P), res[:])
 
         def gather_words(i):
-            nc.vector.tensor_copy(node_words[:, i * 256 : (i + 1) * 256], table_words[:].indirect(picked[:, i * 16 : (i + 1) * 16]))
+            lo, hi = word_cuts[i], word_cuts[i + 1]
+            nc.vector.tensor_copy(node_words[:, lo:hi], table_words[:].indirect(picked[:, lo // 16 : hi // 16]))
 
         nc.vector.tensor_copy(node_scales[:], table_scales[:].indirect(picked[:]))
         quantise(0, False)
         gather_words(0)
         gather_words(1)
-        scores(0, 2)
         quantise(1, False)
-        scores(1, 1)
+        scores(0, 2)
         quantise(2, True)
-        fetch(0, 0, 2)
-        squash(0, 0, 2)
-        fetch(0, 2, 2)
+        scores(1, 1)
         scores(2, 1)
-        squash(0, 2, 2)
-        fetch(1, 0, 2)
         scores(3, 1)
-        squash(1, 0, 2)
+        fetch(0, 0, 2)
+        fetch(0, 2, 2)
+        squash(0, 0, 2)
+        fetch(1, 0, 2)
+        squash(0, 2, 2)
         fetch(1, 2, 2)
-        turn_back(0)
-        squash(1, 2, 2)
+        squash(1, 0, 2)
         fetch(2, 0, 2)
+        squash(1, 2, 2)
         fetch(2, 2, 2)
         squash(2, 0, 2)
-        turn_back(1)
+        turn_back(0)
         fetch(3, 0, 2)
         squash(2, 2, 2)
         fetch(3, 2, 1)
         squash(3, 0, 2)
+        turn_back(1)
         fetch(3, 3, 1)
         squash(3, 2, 1)
         squash(3, 3, 1)
-        for b in range(BLOCKS - 1):
-            pair(b, 0, 2)
-            product(b, 1)
-        turn_back(2, True)
+        pair_blocks(0, 2)
+        pair_blocks(2, 1)
+        product(0, 2)
         pair(3, 0, 1)
+        product(2, 1)
         pair(3, 1, 1)
-        turn_back(3, True)
         product(3, 1)
-        for b in range(BLOCKS):
-            log(b, 1)
-        for b in range(BLOCKS):
-            finish(b)
+        log(0, 1)
+        log(1, 1)
+        turn_back(2)
+        log(2, 1)
+        log(3, 1)
+        finish(0, 1)
+        finish(1, 1)
+        finish(2, 1)
+        finish(3, 1)

@@ -4,11 +4,19 @@ import concourse.mybir as mybir
 from concourse.masks import make_identity
 
 K, T, S, V, U, D = 512, 1024, 512, 512, 256, 4
+FLOPS = 2 * K * V * S
+
 P = 128
 PACK = 4
+QUADRANTS = 4
+LIST_ROWS = 16
 BLOCKS = V // P
 HALVES = U // P
-FLOPS = 2 * K * V * S
+
+LOAD_GROUPS = ((0, 1), (1, 1), (2, 2))
+SUM_GROUPS = ((0, 2), (2, 1), (3, 1))
+WORD_CUTS = (0, 256, 384, 512)
+STEPS = tuple((b, d, 2) for b in range(BLOCKS) for d in (0, 2))[:-1] + ((BLOCKS - 1, 2, 1), (BLOCKS - 1, 3, 1))
 
 F32 = mybir.dt.float32
 BF16 = mybir.dt.bfloat16
@@ -21,6 +29,10 @@ ACT = mybir.ActivationFunctionType
 ALU = mybir.AluOpType
 
 
+def group_of(groups, block):
+    return max(g for g, (first, count) in enumerate(groups) if first <= block)
+
+
 def tile_picked_yhs_nll_p_kernel(tc, x_words, x_scales, hT, turn, offs, pos1, pos2, pos3, pos4, out):
     nc = tc.nc
     with ExitStack() as ctx:
@@ -28,93 +40,75 @@ def tile_picked_yhs_nll_p_kernel(tc, x_words, x_scales, hT, turn, offs, pos1, po
         keep = ctx.enter_context(tc.tile_pool(name="keep", bufs=1))
         psum = ctx.enter_context(tc.psum_pool(name="psum", bufs=1))
 
-        scale_rows = keep.tile([P, T // 4], I32, name="scale_rows")
-        picked = lists.tile([P, S // 16], U16, name="picked")
+        picked = lists.tile([P, S // LIST_ROWS], U16, name="picked")
         nc.sync.dma_start(picked[:], offs)
-        for q in range(4):
+
+        scale_rows = keep.tile([P, T // 4], I32, name="scale_rows")
+        for q in range(QUADRANTS):
             queue = nc.sync if q == 0 else nc.scalar
             queue.dma_start(scale_rows[32 * q : 32 * q + 4, :], x_scales[0, 4 * q : 4 * q + 4, :].bitcast(I32))
         table_scales = keep.tile([P, T], U8, name="table_scales", align_bytes=64)
         nc.vector.memset(table_scales[:].bitcast(I32), 0)
-        for q in range(4):
+        for q in range(QUADRANTS):
             rows = slice(32 * q, 32 * q + 4)
             nc.vector.tensor_copy(table_scales[rows, :].bitcast(I32), scale_rows[rows, :])
+
         zero = keep.tile([P, 1], F32, name="zero")
         nc.vector.memset(zero[:], 0.0)
         half = keep.tile([P, 1], F32, name="half")
         nc.scalar.activation(half[:], zero[:], ACT.Sigmoid)
 
         h_rows = hT.rearrange("(p j) t -> p j t", j=PACK)
-        groups = ((0, 1), (1, 1), (2, 2))
-        h_raw = [keep.tile([P, PACK, n * P], F32, name="h_raw%d" % b) for b, n in groups]
-        paths = [lists.tile([P, U // 16], U16, name="path%d" % d) for d in range(D)]
-        signs = keep.tile([P, D, U], F32, name="signs")
+        h_raw = [keep.tile([P, PACK, count * P], F32, name="h_raw%d" % first) for first, count in LOAD_GROUPS]
         table_words = keep.tile([P, T], U32, name="table_words", align_bytes=64)
-        poss = (pos1, pos2, pos3, pos4)
-
-        def load_h(g):
-            b, n = groups[g]
-            nc.sync.dma_start(h_raw[g][:], h_rows[:, :, b * P : (b + n) * P])
-
-        def load_path(d):
-            nc.sync.dma_start(paths[d][:], poss[d])
-
-        def load_signs():
-            nc.sync.dma_start(signs[:], turn.rearrange("d p u -> p d u"))
-
-        def load_words():
-            nc.sync.dma_start(table_words[:].bitcast(I32), x_words[0].rearrange("p n t -> p (n t)").bitcast(I32))
-
-        load_h(0)
-        load_words()
-        load_h(1)
-        load_h(2)
-        for d in range(D):
-            load_path(d)
-        load_signs()
+        for g, (first, count) in enumerate(LOAD_GROUPS):
+            nc.sync.dma_start(h_raw[g][:], h_rows[:, :, first * P : (first + count) * P])
+            if g == 0:
+                nc.sync.dma_start(table_words[:].bitcast(I32), x_words[0].rearrange("p n j -> p (n j)").bitcast(I32))
+        paths = [lists.tile([P, U // LIST_ROWS], U16, name="path%d" % d) for d in range(D)]
+        for path, pos in zip(paths, (pos1, pos2, pos3, pos4)):
+            nc.sync.dma_start(path[:], pos)
+        signs = [keep.tile([P, 2, U], F32, name="signs%d" % e) for e in range(D // 2)]
+        for e in range(D // 2):
+            nc.sync.dma_start(signs[e][:], turn[2 * e : 2 * e + 2].rearrange("d p r -> p d r"))
 
         ident = keep.tile([P, P], F32, name="ident")
         make_identity(nc, ident[:])
 
         node_scales = keep.tile([P, S], U8, name="node_scales", align_bytes=64)
         node_words = keep.tile([P, S], U32, name="node_words", align_bytes=64)
-        h_words = [keep.tile([P, n * P], U32, name="h_words%d" % b, align_bytes=64) for b, n in groups]
-        h_scales = [keep.tile([P, n * P], U8, name="h_scales%d" % b, align_bytes=64) for b, n in groups]
+        h_words = [keep.tile([P, count * P], U32, name="h_words%d" % first, align_bytes=64) for first, count in LOAD_GROUPS]
+        h_scales = [keep.tile([P, count * P], U8, name="h_scales%d" % first, align_bytes=64) for first, count in LOAD_GROUPS]
         neg_y = [keep.tile([P, S], F32, name="neg_y%d" % b) for b in range(BLOCKS)]
-        pairs = keep.tile([P, BLOCKS, 2, U], F32, name="pairs")
-        prod = keep.tile([P, BLOCKS, U], F32, name="prod")
-        logs = keep.tile([P, BLOCKS, U], F32, name="logs")
-        ramp_banks = [psum.tile([P, 2, U], F32, name="ramp%d" % i) for i in range(BLOCKS // 2)]
         xs = [keep.tile([P, D, U], F32, name="x%d" % b) for b in range(BLOCKS)]
         mags = [keep.tile([P, D, U], F32, name="mag%d" % b) for b in range(BLOCKS)]
-        sigs = keep.tile([P, BLOCKS, 2, 2, U], F32, name="sigs")
-        sum_groups = ((0, 2), (2, 1), (3, 1))
-        sums = {}
-        word_cuts = (0, 256, 512)
+        sigs = keep.tile([P, BLOCKS, D, U], F32, name="sigs")
+        pairs = keep.tile([P, BLOCKS, D // 2, U], F32, name="pairs")
+        prods = keep.tile([P, BLOCKS, U], F32, name="prods")
+        logs = keep.tile([P, BLOCKS, U], F32, name="logs")
 
-        def quantise(g, on_vector):
-            b, n = groups[g]
-            grouped = keep.tile([P, n * P, PACK], BF16, name="grouped%d" % b, align_bytes=64)
-            dst = grouped[:].rearrange("p (c i) j -> p c j i", i=4)
-            src = h_raw[g][:].rearrange("p j (c i) -> p c j i", i=4)
-            if on_vector:
-                nc.vector.tensor_copy(dst, src)
-            else:
-                nc.scalar.copy(dst, src)
+        ramps = [psum.tile([P, 2, U], F32, name="ramps%d" % i) for i in range(BLOCKS // 2)]
+        sums = {}
+
+        def quantise(g, cast):
+            first, count = LOAD_GROUPS[g]
+            grouped = keep.tile([P, count * P, PACK], BF16, name="grouped%d" % first, align_bytes=64)
+            cast(
+                grouped[:].rearrange("p (c i) j -> p c j i", i=4),
+                h_raw[g][:].rearrange("p j (c i) -> p c j i", i=4),
+            )
             nc.vector.quantize_mx(
                 out=h_words[g][:].bitcast(FP8X4),
                 scales=h_scales[g][:],
                 in_=grouped[:].rearrange("p t j -> p (t j)"),
             )
 
-        def scores(b, pieces):
-            g = max(i for i, (first, n) in enumerate(groups) if first <= b)
-            own = slice((b - groups[g][0]) * P, (b - groups[g][0] + 1) * P)
-            cuts = word_cuts if pieces > 1 else (0, S)
+        def scores(b, cuts, first_bank):
+            g = group_of(LOAD_GROUPS, b)
+            own = slice((b - LOAD_GROUPS[g][0]) * P, (b - LOAD_GROUPS[g][0] + 1) * P)
             for i in range(len(cuts) - 1):
-                width = cuts[i + 1] - cuts[i]
                 cols = slice(cuts[i], cuts[i + 1])
-                y_bank = psum.tile([P, width], F32, name="y_bank", tag="y_bank", bufs=2)
+                y_bank = psum.tile([P, cuts[i + 1] - cuts[i]], F32, name="y_bank", tag="bank%d" % (first_bank + i))
                 nc.tensor.matmul_mx(
                     out=y_bank[:],
                     lhsT=h_words[g][:, own].bitcast(FP8X4),
@@ -127,118 +121,80 @@ def tile_picked_yhs_nll_p_kernel(tc, x_words, x_scales, hT, turn, offs, pos1, po
                 nc.scalar.activation(neg_y[b][:, cols], y_bank[:], ACT.Copy, scale=-1.0)
 
         def fetch(b, d0, count):
-            x, mag = xs[b], mags[b]
-            i = max(j for j, (first, n) in enumerate(sum_groups) if first <= b)
-            first, n = sum_groups[i]
-            if d0 == 0 and b == first:
-                if i == len(sum_groups) - 1:
-                    sums[i] = [psum.tile([P, n, P], F32, name="sum_last", tag="y_bank", bufs=2) for h in range(HALVES)]
-                else:
-                    sums[i] = [psum.tile([P, n, P], F32, name="sum%d_%d" % (i, h)) for h in range(HALVES)]
+            g = group_of(SUM_GROUPS, b)
+            first, blocks = SUM_GROUPS[g]
+            if g not in sums:
+                sums[g] = [
+                    psum.tile([P, blocks, P], F32, name="sums", tag="bank%d" % (HALVES * g + h)) for h in range(HALVES)
+                ]
             for d in range(d0, d0 + count):
-                nc.vector.tensor_tensor(x[:, d, :], neg_y[b][:].indirect(paths[d][:]), signs[:, d, :], ALU.mult)
-            nc.scalar.activation(mag[:, d0 : d0 + count, :], x[:, d0 : d0 + count, :], ACT.Abs)
-            for terms in (x, mag):
+                nc.vector.tensor_tensor(xs[b][:, d, :], neg_y[b][:].indirect(paths[d][:]), signs[d // 2][:, d % 2, :], ALU.mult)
+            nc.scalar.activation(mags[b][:, d0 : d0 + count, :], xs[b][:, d0 : d0 + count, :], ACT.Abs)
+            for of_mags, terms in enumerate((xs[b], mags[b])):
                 for d in range(d0, d0 + count):
                     for h in range(HALVES):
                         nc.tensor.matmul(
-                            sums[i][h][:, b - first, :],
+                            sums[g][h][:, b - first, :],
                             terms[:, d, h * P : (h + 1) * P],
                             ident[:],
-                            start=(terms is x and d == 0),
-                            stop=(terms is mag and d == D - 1),
+                            start=(d == 0 and not of_mags),
+                            stop=(d == D - 1 and bool(of_mags)),
                             is_transpose=True,
                         )
 
         def squash(b, d0, count):
-            sig = sigs[:, b].rearrange("p e f u -> p (e f) u")
-            nc.scalar.activation(sig[:, d0 : d0 + count, :], mags[b][:, d0 : d0 + count, :], ACT.Sigmoid)
+            nc.scalar.activation(sigs[:, b, d0 : d0 + count, :], mags[b][:, d0 : d0 + count, :], ACT.Sigmoid)
 
-        def clock(src, n):
-            c = keep.tile([P, 1], F32, name="clock%d" % n)
-            nc.gpsimd.tensor_copy(c[:], src)
-
-        def pair(b, e0, count):
-            es = slice(e0, e0 + count)
-            nc.vector.tensor_tensor(pairs[:, b, es, :], sigs[:, b, es, 0, :], sigs[:, b, es, 1, :], ALU.mult)
-
-        def pair_blocks(b0, count):
-            bs = slice(b0, b0 + count)
-            nc.vector.tensor_tensor(pairs[:, bs], sigs[:, bs, :, 0, :], sigs[:, bs, :, 1, :], ALU.mult)
-
-        def product(b0, count):
-            bs = slice(b0, b0 + count)
-            nc.vector.tensor_tensor(prod[:, bs, :], pairs[:, bs, 0, :], pairs[:, bs, 1, :], ALU.mult)
-
-        def turn_back(i, on_vector=False):
-            first, n = sum_groups[i]
-            turned = keep.tile([P, HALVES, n, P], F32, name="turned%d" % i)
+        def turn_back(g, copy):
+            first, blocks = SUM_GROUPS[g]
+            turned = keep.tile([P, HALVES, blocks, P], F32, name="turned%d" % g)
             for h in range(HALVES):
-                if on_vector:
-                    nc.vector.tensor_copy(turned[:, h], sums[i][h][:])
-                else:
-                    nc.scalar.copy(turned[:, h], sums[i][h][:])
-                for k in range(n):
-                    b = first + k
-                    nc.tensor.transpose(ramp_banks[b // 2][:, b % 2, h * P : (h + 1) * P], turned[:, h, k, :], ident[:])
+                copy(turned[:, h], sums[g][h][:])
+                for b in range(first, first + blocks):
+                    nc.tensor.transpose(ramps[b // 2][:, b % 2, h * P : (h + 1) * P], turned[:, h, b - first, :], ident[:])
 
-        def log(b0, count):
-            bs = slice(b0, b0 + count)
-            nc.scalar.activation(logs[:, bs, :], prod[:, bs, :], ACT.Ln)
+        def multiply_pairs(g):
+            first, blocks = SUM_GROUPS[g]
+            by_pair = sigs[:, first : first + blocks].rearrange("p b (e f) r -> p b e f r", f=2)
+            nc.vector.tensor_tensor(pairs[:, first : first + blocks], by_pair[:, :, :, 0, :], by_pair[:, :, :, 1, :], ALU.mult)
 
-        def finish(b0, count):
-            res = keep.tile([P, count, U], F32, name="res%d" % b0)
-            ks = slice(b0 % 2, b0 % 2 + count)
-            nc.vector.scalar_tensor_tensor(res[:], ramp_banks[b0 // 2][:, ks, :], half[:], logs[:, b0 : b0 + count, :], ALU.mult, ALU.subtract)
-            nc.sync.dma_start(out[b0 * P : (b0 + count) * P, :].rearrange("(b p) u -> p b u", p=P), res[:])
-
-        def gather_words(i):
-            lo, hi = word_cuts[i], word_cuts[i + 1]
-            nc.vector.tensor_copy(node_words[:, lo:hi], table_words[:].indirect(picked[:, lo // 16 : hi // 16]))
+        def multiply_all(g):
+            first, blocks = SUM_GROUPS[g]
+            own = slice(first, first + blocks)
+            nc.vector.tensor_tensor(prods[:, own, :], pairs[:, own, 0, :], pairs[:, own, 1, :], ALU.mult)
 
         nc.vector.tensor_copy(node_scales[:], table_scales[:].indirect(picked[:]))
-        quantise(0, False)
-        gather_words(0)
-        gather_words(1)
-        quantise(1, False)
-        scores(0, 2)
-        quantise(2, True)
-        scores(1, 1)
-        scores(2, 1)
-        scores(3, 1)
-        fetch(0, 0, 2)
-        fetch(0, 2, 2)
-        squash(0, 0, 2)
-        fetch(1, 0, 2)
-        squash(0, 2, 2)
-        fetch(1, 2, 2)
-        squash(1, 0, 2)
-        fetch(2, 0, 2)
-        squash(1, 2, 2)
-        fetch(2, 2, 2)
-        squash(2, 0, 2)
-        turn_back(0)
-        fetch(3, 0, 2)
-        squash(2, 2, 2)
-        fetch(3, 2, 1)
-        squash(3, 0, 2)
-        turn_back(1)
-        fetch(3, 3, 1)
-        squash(3, 2, 1)
-        squash(3, 3, 1)
-        pair_blocks(0, 2)
-        pair_blocks(2, 1)
-        product(0, 2)
-        pair(3, 0, 1)
-        product(2, 1)
-        pair(3, 1, 1)
-        product(3, 1)
-        log(0, 1)
-        log(1, 1)
-        turn_back(2)
-        log(2, 1)
-        log(3, 1)
-        finish(0, 1)
-        finish(1, 1)
-        finish(2, 1)
-        finish(3, 1)
+        quantise(0, nc.scalar.copy)
+        for lo, hi in zip(WORD_CUTS, WORD_CUTS[1:]):
+            nc.vector.tensor_copy(node_words[:, lo:hi], table_words[:].indirect(picked[:, lo // LIST_ROWS : hi // LIST_ROWS]))
+        quantise(1, nc.scalar.copy)
+        scores(0, WORD_CUTS, 0)
+        quantise(2, nc.vector.tensor_copy)
+        for b in range(1, BLOCKS):
+            scores(b, (0, S), len(WORD_CUTS) - 2 + b)
+
+        for step, following in zip(STEPS, STEPS[1:]):
+            if step == STEPS[0]:
+                fetch(*step)
+            fetch(*following)
+            squash(*step)
+            b, d0, count = step
+            g = group_of(SUM_GROUPS, b)
+            if g > 0 and b == SUM_GROUPS[g][0] and d0 == 0:
+                turn_back(g - 1, nc.scalar.copy)
+        squash(*STEPS[-1])
+
+        last = len(SUM_GROUPS) - 1
+        for g in range(last):
+            multiply_pairs(g)
+        for g in range(last):
+            multiply_all(g)
+        multiply_pairs(last)
+        turn_back(last, nc.vector.tensor_copy)
+        multiply_all(last)
+        for b in range(BLOCKS):
+            nc.scalar.activation(logs[:, b, :], prods[:, b, :], ACT.Ln)
+        for b in range(BLOCKS):
+            result = keep.tile([P, U], F32, name="result%d" % b)
+            nc.vector.scalar_tensor_tensor(result[:], ramps[b // 2][:, b % 2, :], half[:], logs[:, b, :], ALU.mult, ALU.subtract)
+            nc.sync.dma_start(out[b * P : (b + 1) * P, :], result[:])

@@ -45,7 +45,7 @@ def tile_picked_yhs_nll_p_kernel(tc, x_words, x_scales, hT, turn, offs, pos1, po
 
         scale_rows = keep.tile([P, T // 4], I32, name="scale_rows")
         for q in range(QUADRANTS):
-            queue = nc.sync if q == 0 else nc.scalar
+            queue = nc.sync if q < QUADRANTS // 2 else nc.scalar
             queue.dma_start(scale_rows[32 * q : 32 * q + 4, :], x_scales[0, 4 * q : 4 * q + 4, :].bitcast(I32))
         table_scales = keep.tile([P, T], U8, name="table_scales", align_bytes=64)
         nc.vector.memset(table_scales[:].bitcast(I32), 0)

from contextlib import ExitStack

import concourse.mybir as mybir
from concourse.masks import make_identity

K, T, S, V, U, D = 512, 1024, 512, 512, 256, 4
FLOPS = 2 * K * V * S

P = 128
PACK = 4
QUADRANTS = 4
LIST_ROWS = 16
BLOCKS = V // P
HALVES = U // P

LOAD_GROUPS = ((0, 1), (1, 1), (2, 2))
SUM_GROUPS = ((0, 2), (2, 1), (3, 1))
WORD_CUTS = (0, 256, 384, 512)
STEPS = tuple((b, d, 2) for b in range(BLOCKS) for d in (0, 2))[:-1] + ((BLOCKS - 1, 2, 1), (BLOCKS - 1, 3, 1))

F32 = mybir.dt.float32
BF16 = mybir.dt.bfloat16
I32 = mybir.dt.int32
U32 = mybir.dt.uint32
U16 = mybir.dt.uint16
U8 = mybir.dt.uint8
FP8X4 = mybir.dt.float8_e4m3fn_x4
ACT = mybir.ActivationFunctionType
ALU = mybir.AluOpType


def group_of(groups, block):
    return max(g for g, (first, count) in enumerate(groups) if first <= block)


def tile_picked_yhs_nll_p_kernel(tc, x_words, x_scales, hT, turn, offs, pos1, pos2, pos3, pos4, out):
    nc = tc.nc
    with ExitStack() as ctx:
        lists = ctx.enter_context(tc.tile_pool(name="lists", bufs=1))
        keep = ctx.enter_context(tc.tile_pool(name="keep", bufs=1))
        psum = ctx.enter_context(tc.psum_pool(name="psum", bufs=1))

        picked = lists.tile([P, S // LIST_ROWS], U16, name="picked")
        nc.sync.dma_start(picked[:], offs)

        scale_rows = keep.tile([P, T // 4], I32, name="scale_rows")
        for q in range(QUADRANTS):
            queue = nc.sync if q < QUADRANTS // 2 else nc.scalar
            queue.dma_start(scale_rows[32 * q : 32 * q + 4, :], x_scales[0, 4 * q : 4 * q + 4, :].bitcast(I32))
        table_scales = keep.tile([P, T], U8, name="table_scales", align_bytes=64)
        nc.vector.memset(table_scales[:].bitcast(I32), 0)
        for q in range(QUADRANTS):
            rows = slice(32 * q, 32 * q + 4)
            nc.vector.tensor_copy(table_scales[rows, :].bitcast(I32), scale_rows[rows, :])

        zero = keep.tile([P, 1], F32, name="zero")
        nc.vector.memset(zero[:], 0.0)
        half = keep.tile([P, 1], F32, name="half")
        nc.scalar.activation(half[:], zero[:], ACT.Sigmoid)

        h_rows = hT.rearrange("(p j) t -> p j t", j=PACK)
        h_raw = [keep.tile([P, PACK, count * P], F32, name="h_raw%d" % first) for first, count in LOAD_GROUPS]
        table_words = keep.tile([P, T], U32, name="table_words", align_bytes=64)
        for g, (first, count) in enumerate(LOAD_GROUPS):
            nc.sync.dma_start(h_raw[g][:], h_rows[:, :, first * P : (first + count) * P])
            if g == 0:
                nc.sync.dma_start(table_words[:].bitcast(I32), x_words[0].rearrange("p n j -> p (n j)").bitcast(I32))
        paths = [lists.tile([P, U // LIST_ROWS], U16, name="path%d" % d) for d in range(D)]
        for path, pos in zip(paths, (pos1, pos2, pos3, pos4)):
            nc.sync.dma_start(path[:], pos)
        signs = [keep.tile([P, 2, U], F32, name="signs%d" % e) for e in range(D // 2)]
        for e in range(D // 2):
            nc.sync.dma_start(signs[e][:], turn[2 * e : 2 * e + 2].rearrange("d p r -> p d r"))

        ident = keep.tile([P, P], F32, name="ident")
        make_identity(nc, ident[:])

        node_scales = keep.tile([P, S], U8, name="node_scales", align_bytes=64)
        node_words = keep.tile([P, S], U32, name="node_words", align_bytes=64)
        h_words = [keep.tile([P, count * P], U32, name="h_words%d" % first, align_bytes=64) for first, count in LOAD_GROUPS]
        h_scales = [keep.tile([P, count * P], U8, name="h_scales%d" % first, align_bytes=64) for first, count in LOAD_GROUPS]
        neg_y = [keep.tile([P, S], F32, name="neg_y%d" % b) for b in range(BLOCKS)]
        xs = [keep.tile([P, D, U], F32, name="x%d" % b) for b in range(BLOCKS)]
        mags = [keep.tile([P, D, U], F32, name="mag%d" % b) for b in range(BLOCKS)]
        sigs = keep.tile([P, BLOCKS, D, U], F32, name="sigs")
        pairs = keep.tile([P, BLOCKS, D // 2, U], F32, name="pairs")
        prods = keep.tile([P, BLOCKS, U], F32, name="prods")
        logs = keep.tile([P, BLOCKS, U], F32, name="logs")

        ramps = [psum.tile([P, 2, U], F32, name="ramps%d" % i) for i in range(BLOCKS // 2)]
        sums = {}

        def quantise(g, cast):
            first, count = LOAD_GROUPS[g]
            grouped = keep.tile([P, count * P, PACK], BF16, name="grouped%d" % first, align_bytes=64)
            cast(
                grouped[:].rearrange("p (c i) j -> p c j i", i=4),
                h_raw[g][:].rearrange("p j (c i) -> p c j i", i=4),
            )
            nc.vector.quantize_mx(
                out=h_words[g][:].bitcast(FP8X4),
                scales=h_scales[g][:],
                in_=grouped[:].rearrange("p t j -> p (t j)"),
            )

        def scores(b, cuts, first_bank):
            g = group_of(LOAD_GROUPS, b)
            own = slice((b - LOAD_GROUPS[g][0]) * P, (b - LOAD_GROUPS[g][0] + 1) * P)
            for i in range(len(cuts) - 1):
                cols = slice(cuts[i], cuts[i + 1])
                y_bank = psum.tile([P, cuts[i + 1] - cuts[i]], F32, name="y_bank", tag="bank%d" % (first_bank + i))
                nc.tensor.matmul_mx(
                    out=y_bank[:],
                    lhsT=h_words[g][:, own].bitcast(FP8X4),
                    lhsT_scale=h_scales[g][:, own],
                    rhs=node_words[:, cols].bitcast(FP8X4),
                    rhs_scale=node_scales[:, cols],
                    start=True,
                    stop=True,
                )
                nc.scalar.activation(neg_y[b][:, cols], y_bank[:], ACT.Copy, scale=-1.0)

        def fetch(b, d0, count):
            g = group_of(SUM_GROUPS, b)
            first, blocks = SUM_GROUPS[g]
            if g not in sums:
                sums[g] = [
                    psum.tile([P, blocks, P], F32, name="sums", tag="bank%d" % (HALVES * g + h)) for h in range(HALVES)
                ]
            for d in range(d0, d0 + count):
                nc.vector.tensor_tensor(xs[b][:, d, :], neg_y[b][:].indirect(paths[d][:]), signs[d // 2][:, d % 2, :], ALU.mult)
            nc.scalar.activation(mags[b][:, d0 : d0 + count, :], xs[b][:, d0 : d0 + count, :], ACT.Abs)
            for of_mags, terms in enumerate((xs[b], mags[b])):
                for d in range(d0, d0 + count):
                    for h in range(HALVES):
                        nc.tensor.matmul(
                            sums[g][h][:, b - first, :],
                            terms[:, d, h * P : (h + 1) * P],
                            ident[:],
                            start=(d == 0 and not of_mags),
                            stop=(d == D - 1 and bool(of_mags)),
                            is_transpose=True,
                        )

        def squash(b, d0, count):
            nc.scalar.activation(sigs[:, b, d0 : d0 + count, :], mags[b][:, d0 : d0 + count, :], ACT.Sigmoid)

        def turn_back(g, copy):
            first, blocks = SUM_GROUPS[g]
            turned = keep.tile([P, HALVES, blocks, P], F32, name="turned%d" % g)
            for h in range(HALVES):
                copy(turned[:, h], sums[g][h][:])
                for b in range(first, first + blocks):
                    nc.tensor.transpose(ramps[b // 2][:, b % 2, h * P : (h + 1) * P], turned[:, h, b - first, :], ident[:])

        def multiply_pairs(g):
            first, blocks = SUM_GROUPS[g]
            by_pair = sigs[:, first : first + blocks].rearrange("p b (e f) r -> p b e f r", f=2)
            nc.vector.tensor_tensor(pairs[:, first : first + blocks], by_pair[:, :, :, 0, :], by_pair[:, :, :, 1, :], ALU.mult)

        def multiply_all(g):
            first, blocks = SUM_GROUPS[g]
            own = slice(first, first + blocks)
            nc.vector.tensor_tensor(prods[:, own, :], pairs[:, own, 0, :], pairs[:, own, 1, :], ALU.mult)

        nc.vector.tensor_copy(node_scales[:], table_scales[:].indirect(picked[:]))
        quantise(0, nc.scalar.copy)
        for lo, hi in zip(WORD_CUTS, WORD_CUTS[1:]):
            nc.vector.tensor_copy(node_words[:, lo:hi], table_words[:].indirect(picked[:, lo // LIST_ROWS : hi // LIST_ROWS]))
        quantise(1, nc.scalar.copy)
        scores(0, WORD_CUTS, 0)
        quantise(2, nc.vector.tensor_copy)
        for b in range(1, BLOCKS):
            scores(b, (0, S), len(WORD_CUTS) - 2 + b)

        for step, following in zip(STEPS, STEPS[1:]):
            if step == STEPS[0]:
                fetch(*step)
            fetch(*following)
            squash(*step)
            b, d0, count = step
            g = group_of(SUM_GROUPS, b)
            if g > 0 and b == SUM_GROUPS[g][0] and d0 == 0:
                turn_back(g - 1, nc.scalar.copy)
        squash(*STEPS[-1])

        last = len(SUM_GROUPS) - 1
        for g in range(last):
            multiply_pairs(g)
        for g in range(last):
            multiply_all(g)
        multiply_pairs(last)
        turn_back(last, nc.vector.tensor_copy)
        multiply_all(last)
        for b in range(BLOCKS):
            nc.scalar.activation(logs[:, b, :], prods[:, b, :], ACT.Ln)
        for b in range(BLOCKS):
            result = keep.tile([P, U], F32, name="result%d" % b)
            nc.vector.scalar_tensor_tensor(result[:], ramps[b // 2][:, b % 2, :], half[:], logs[:, b, :], ALU.mult, ALU.subtract)
            nc.sync.dma_start(out[b * P : (b + 1) * P, :], result[:])
